import numpy as np, ml_dtypes
CORES = [16,17,18,19,150,151]
N = 6
import mx_ref
NC, G, MB = 128, 2, 3
C = np.float32(0.031)
BF = ml_dtypes.bfloat16
def cut(t, i, w=512):
    return t[:, w * i:w * i + w]
def tile(rs):
    return np.stack(rs, axis=2).reshape(128, -1).astype(BF)
def layer(w, X):
    out = []
    for i in range(G):
        for t in range(len(X)):
            p = mx_ref.matmul(mx_ref.quantize(cut(w, len(X) * i + t)), X[t])
            z = p if t == 0 else z + p
        out.append(z)
    return out
def act(Z):
    return [np.maximum(s * z, 0) * C for z in Z for s in (1, -1)]
def masked(U, Z):
    return [(s * u * (s * z > 0)) * C for u, z in zip(U, Z) for s in (1, -1)]
def setup_inputs(rng):
    def f(*shape):
        return mx_ref.flush((rng.standard_normal(shape, dtype=np.float32) * np.exp2(rng.integers(-2, 3, shape[:-1] + (1,)))).astype(BF))
    return {"x": f(N, 128, MB * 4 * NC), "e": f(N, 128, MB * 4 * NC), "w": f(N, 128, G * 512), "v": f(N, 128, G * 512)}
def setup_inputs_blocks(rng):
    d = setup_inputs(rng)
    for k in ("x", "e"): d[k] = mx_ref.spread(d[k], rng, 4)
    for k in ("w", "v"): d[k] = mx_ref.spread(d[k], rng, 1)
    return d
def setup_inputs_wide(rng):
    d = setup_inputs(rng)
    for k in ("x", "e"): d[k] = mx_ref.flush((d[k].astype(np.float32) * np.exp2(rng.integers(-8, 9, (N, 1, 1))).astype(np.float32)).astype(BF))
    return d
def setup_inputs_zeros(rng):
    d = setup_inputs(rng); v = d["x"].reshape(N, 128, -1, 4).copy()
    v[np.broadcast_to((rng.random((N, 1, v.shape[2], 1)) < 0.33), v.shape)] = 0
    d["x"] = v.reshape(d["x"].shape)
    return d
def reference(x, e, w, v):
    y = np.full((N, 128, MB * G * NC), np.nan, np.float32)
    for m in range(MB):
        a = mx_ref.quantize(cut(x[N - 1], m, 4 * NC)); Z = []
        for s in range(N):
            Z.append(layer(w[s], [a]))
            if s < N - 1: a = mx_ref.quantize(tile(act(Z[s])))
        b = mx_ref.quantize(cut(e[0], m, 4 * NC))
        for s in range(N - 1, 0, -1):
            b = mx_ref.quantize(tile(masked(layer(v[s], [b]), Z[s])))
        U = layer(v[0], [b])
        for i in range(G):
            y[0][:, NC * (G * m + i):NC * (G * m + i) + NC] = U[i] * (Z[0][i] > 0)
    return {"y": y}

import numpy as np
from concourse.bass import DstId, RemoteDMATransfer
from concourse.mybir import dt, AluOpType, ActivationFunctionType

C = float(np.float32(0.031))
NC = 128
MB = 3
Q = NC // 4

F8, U8, BF, F32 = "float8_e4m3fn_x4", "uint8", "bfloat16", "float32"
SCRATCH = {
    "xt": ("sbuf", [128, 4 * NC * MB], BF),
    "wt": ("sbuf", [128, 1024], BF), "vt": ("sbuf", [128, 1024], BF),
    "xq": ("sbuf", [128, NC * MB], F8), "xs": ("sbuf", [128, NC * MB], U8),
    "wq": ("sbuf", [128, 256], F8), "ws": ("sbuf", [128, 256], U8),
    "vq": ("sbuf", [128, 256], F8), "vs": ("sbuf", [128, 256], U8),
    "aqi": ("sbuf", [128, NC * MB], F8), "asi": ("sbuf", [128, NC * MB], U8),
    "aqo": ("sbuf", [128, NC * MB], F8), "aso": ("sbuf", [128, NC * MB], U8),
    "bqi": ("sbuf", [128, NC * MB], F8), "bsi": ("sbuf", [128, NC * MB], U8),
    "bqo": ("sbuf", [128, NC * MB], F8), "bso": ("sbuf", [128, NC * MB], U8),
    "rq": ("sbuf", [128, NC], F8), "rs": ("sbuf", [128, NC], U8),
    "ha": ("sbuf", [128, 4 * NC * MB], BF), "hb": ("sbuf", [128, 4 * NC * MB], BF),
    "f": ("sbuf", [128, 4 * NC * MB], F32),
    "sg": ("sbuf", [128, NC * MB], F32),
    "yt": ("sbuf", [128, 2 * NC * MB], F32),
    "ps": ("psum", [128, 512 * 8], F32),
}
_PER = ["aa", "ba", "z0", "z1", "u0", "u1", "sa", "sv", "qa", "mk", "sb", "qb", "ma", "mb", "md", "sg", "sf", "y0", "y1"]
SEMAPHORES = ["lx0", "lx1", "lw", "lv", "qx0", "qx1", "qx2", "qw", "qv", "ra", "rb", "sent", "st0", "st1"] + [
    "%s_%d" % (p, m) for p in _PER for m in range(MB)]


def rank_program(g, core, T, topo):
    rank = T.rank_of(core)
    if rank is None:
        return
    R = list(T.cores)
    N = len(R)
    A, ACT = AluOpType, ActivationFunctionType
    last = N - 1
    sent = [0]

    def S(name, m):
        return T.sem["%s_%d" % (name, m)]

    def engines(src, dst):
        k = topo.mask(R[src], R[dst])
        return [b for b in range(k.bit_length()) if (k >> b) & 1]

    def bits(es):
        return sum(1 << b for b in es)

    def codes(buf, a, b):
        return T[buf][:, a:b].bitcast(dt.uint8)

    def plane(buf, a, b):
        return T[buf][:, a:b]

    def send(dst, out, in_, sem, es):
        rid, pid = topo.addr(R[dst], core)
        g.remote_dma(out, in_, sem, T.sem.sent, pid, rid, bits(es))
        sent[0] += len(es)

    def split(src, dst, way, m):
        es = engines(src, dst)
        if way == "b" and m == 0:
            down = engines(src, (src + 1) % N)
            rest = [b for b in es if b not in down]
            if rest:
                return [b for b in es if b in down], rest
        return es, es

    def send_tile(dst, way, m, src_bufs):
        c, p = split(rank, dst, way, m)
        a, b = NC * m, NC * m + NC
        sem = S(way + "a", m)
        send(dst, codes(way + "qi", a, b), codes(src_bufs[0], a, b), sem, c)
        send(dst, plane(way + "si", a, b), plane(src_bufs[1], a, b), sem, p)

    def arrive(src, way, m):
        c, p = split(src, rank, way, m)
        return len(c) + len(p)

    off = engines(0, last)
    pool = off + [b for b in engines(0, 1) if b not in off]
    piece = {last: pool[0:2], 4: pool[2:4], 3: pool[4:8], 1: pool[8:12], 2: pool[12:16]}
    quarter = {1: 0, 2: 1, 3: 2, last: 3}
    e0_count = len(piece[last]) + 2 * len(engines(3, last)) + len(engines(4, last))
    e12_count = 2 * len(engines(0, last))

    def bank(k):
        return T.ps[:, 512 * k:512 * k + NC]

    def zbank(m, i):
        if rank == last:
            return bank((4, 6, 4)[m] + i)
        return bank(2 * m + i)

    def ubank(m, i):
        if rank == last:
            return bank((0, 2, 0)[m] + i)
        return bank((6, 0, 2)[m] + i)

    def mask(m, b):
        return T.f[:, NC * (4 * m + b):NC * (4 * m + b) + NC]

    def col(buf, m, b):
        return T[buf][:, 4 * NC * m + b:4 * NC * (m + 1):4]

    W1 = 4 * NC

    def load(out, in_, sem):
        g.sync.dma_start(out, in_).then_inc(sem, 16)

    def quant_in(q, s, t, a, b, lsem, qsem):
        g.vector.wait_ge(lsem, 16)
        g.vector.quantize_mx(T[q][:, a:b], T[s][:, a:b], T[t][:, 4 * a:4 * b]).then_inc(qsem, 1)

    sem = T.sem
    if rank == last:
        load(T.xt[:, 0:W1], T.x[:, 0:W1], sem.lx0)
        load(T.xt[:, W1:MB * W1], T.x[:, W1:MB * W1], sem.lx1)
        load(T.wt[:], T.w[:], sem.lw)
        load(T.vt[:], T.v[:], sem.lv)
        quant_in("xq", "xs", "xt", 0, NC, sem.lx0, sem.qx0)
        quant_in("xq", "xs", "xt", NC, 2 * NC, sem.lx1, sem.qx1)
        quant_in("xq", "xs", "xt", 2 * NC, 3 * NC, sem.lx1, sem.qx2)
        quant_in("wq", "ws", "wt", 0, 256, sem.lw, sem.qw)
        quant_in("vq", "vs", "vt", 0, 256, sem.lv, sem.qv)
    elif rank == 0:
        load(T.xt[:, 0:W1], T.e[:, 0:W1], sem.lx0)
        load(T.wt[:], T.w[:], sem.lw)
        load(T.xt[:, W1:MB * W1], T.e[:, W1:MB * W1], sem.lx1)
        load(T.vt[:], T.v[:], sem.lv)
        quant_in("xq", "xs", "xt", 0, NC, sem.lx0, sem.qx0)
        quant_in("wq", "ws", "wt", 0, 256, sem.lw, sem.qw)
    else:
        load(T.wt[:], T.w[:], sem.lw)
        load(T.vt[:], T.v[:], sem.lv)
        quant_in("wq", "ws", "wt", 0, 256, sem.lw, sem.qw)
        quant_in("vq", "vs", "vt", 0, 256, sem.lv, sem.qv)

    if rank == last:
        for m in range(MB):
            g.wait_ge(sem["qx%d" % m], 1)
            send_tile(0, "a", m, ("xq", "xs"))
    elif rank == 0:
        g.wait_ge(sem.qx0, 1)
        tr = []
        for d in (1, 2, 3, 4, last):
            rid, pid = topo.addr(R[d], core)
            if d == 4:
                s_, d_, rsem = plane("xs", 0, NC), plane("rs", 0, NC), sem.ra
            else:
                k = quarter[d]
                s_ = codes("xq", Q * k, Q * k + Q)
                d_ = codes("bqi" if d == last else "rq", Q * k, Q * k + Q)
                rsem = S("ba", 0) if d == last else sem.ra
            tr.append(RemoteDMATransfer(dst_ids=[DstId(rid=rid, pnc=pid)], dma_engine_mask=bits(piece[d]),
                                        remote_sem=rsem, src=s_, dst=d_))
            sent[0] += len(piece[d])
        g.remote_dma_fused(tr, local_sem=sem.sent)
    else:
        g.wait_ge(sem.ra, len(piece[rank]))
        if rank in (1, 2):
            k = quarter[rank]
            send(3, codes("rq", Q * k, Q * k + Q), codes("rq", Q * k, Q * k + Q), sem.rb, engines(rank, 3))
        elif rank == 3:
            k = quarter[3]
            send(last, codes("bqi", Q * k, Q * k + Q), codes("rq", Q * k, Q * k + Q), S("ba", 0), engines(3, last))
            g.wait_ge(sem.rb, len(engines(1, 3)) + len(engines(2, 3)))
            send(last, codes("bqi", 0, 2 * Q), codes("rq", 0, 2 * Q), S("ba", 0), engines(3, last))
        else:
            send(last, plane("bsi", 0, NC), plane("rs", 0, NC), S("ba", 0), engines(4, last))
    if rank < last:
        for m in range(MB):
            g.wait_ge(S("qa", m), 1)
            send_tile(rank + 1, "a", m, ("aqo", "aso"))
    if rank == 0:
        es = engines(0, last)
        g.wait_ge(sem.qx1, 1)
        send(last, codes("bqi", NC, 3 * NC), codes("xq", NC, 3 * NC), S("ba", 1), es)
        send(last, plane("bsi", NC, 3 * NC), plane("xs", NC, 3 * NC), S("ba", 1), es)
    if rank > 0:
        for m in range(MB):
            g.wait_ge(S("qb", m), 1)
            send_tile(rank - 1, "b", m, ("bqo", "bso"))
    g.wait_ge(sem.sent, sent[0])

    def products(q, s, inq, ins, m, out, name):
        a, b = NC * m, NC * m + NC
        for i in range(2):
            g.tensor.matmul_mx(out(m, i), T[q][:, 128 * i:128 * i + 128], T[s][:, 128 * i:128 * i + 128],
                               T[inq][:, a:b], T[ins][:, a:b], True, True).then_inc(S("%s%d" % (name, i), m), 1)

    def down(m):
        g.tensor.wait_ge(S("aa", m), arrive((rank - 1) % N, "a", m))
        products("wq", "ws", "aqi", "asi", m, zbank, "z")

    def back(m):
        if rank < last:
            g.tensor.wait_ge(S("ba", m), arrive(rank + 1, "b", m))
            if m > 0:
                g.tensor.wait_ge(S("mk", m - 1), 2 if rank == 0 else 4)
        elif m < 2:
            g.tensor.wait_ge(S("ba", m), (e0_count, e12_count)[m])
        else:
            g.tensor.wait_ge(S("sb", 0), 4)
        products("vq", "vs", "bqi", "bsi", m, ubank, "u")

    if rank == last:
        g.tensor.wait_ge(sem.qv, 1)
        g.tensor.wait_ge(sem.qw, 1)
        for m in range(MB):
            back(m)
            down(m)
    else:
        g.tensor.wait_ge(sem.qw, 1)
        for m in range(MB):
            down(m)
        g.tensor.wait_ge(sem.qv, 1)
        for m in range(MB):
            back(m)

    V = g.vector

    def quant_tile(t, q, s, m, qsem):
        a, b = NC * m, NC * m + NC
        V.quantize_mx(T[q][:, a:b], T[s][:, a:b], T[t][:, 4 * a:4 * b]).then_inc(qsem, 1)

    if rank == last:
        for m in range(MB):
            sg = T.sg[:, NC * m:NC * m + NC]
            g.scalar.wait_ge(S("z1", m), 1)
            g.scalar.activation(sg, zbank(m, 1), ACT.Sign).then_inc(S("sg", m), 1)
            g.scalar.wait_ge(S("sg", m), 1)
            g.scalar.activation(mask(m, 2), sg, ACT.Relu, scale=C).then_inc(S("sf", m), 1)

            V.wait_ge(S("z0", m), 1)
            V.tensor_scalar(mask(m, 0), zbank(m, 0), 0.0, C, A.is_gt, A.mult).then_inc(S("ma", m), 1)
            V.tensor_scalar(mask(m, 1), zbank(m, 0), 0.0, -C, A.is_lt, A.mult).then_inc(S("mb", m), 1)
            V.wait_ge(S("u0", m), 1)
            V.wait_ge(S("ma", m), 1)
            V.tensor_tensor(col("hb", m, 0), ubank(m, 0), mask(m, 0), A.mult).then_inc(S("sb", m), 1)
            V.wait_ge(S("mb", m), 1)
            V.tensor_tensor(col("hb", m, 1), ubank(m, 0), mask(m, 1), A.mult).then_inc(S("sb", m), 1)
            V.wait_ge(S("sg", m), 1)
            V.tensor_scalar(mask(m, 3), zbank(m, 1), 0.0, -C, A.is_lt, A.mult).then_inc(S("md", m), 1)
            V.wait_ge(S("u1", m), 1)
            V.wait_ge(S("sf", m), 1)
            V.tensor_tensor(col("hb", m, 2), ubank(m, 1), mask(m, 2), A.mult).then_inc(S("sb", m), 1)
            V.wait_ge(S("md", m), 1)
            V.tensor_tensor(col("hb", m, 3), ubank(m, 1), mask(m, 3), A.mult).then_inc(S("sb", m), 1)
            V.wait_ge(S("sb", m), 4)
            quant_tile("hb", "bqo", "bso", m, S("qb", m))
        return

    for m in range(MB):
        g.scalar.wait_ge(S("z0", m), 1)
        g.scalar.activation(col("ha", m, 0), zbank(m, 0), ACT.Relu, scale=C).then_inc(S("sa", m), 1)
        g.scalar.activation(col("ha", m, 1), zbank(m, 0), ACT.Relu, scale=-C).then_inc(S("sa", m), 1)
        V.wait_ge(S("z1", m), 1)
        V.tensor_scalar(col("ha", m, 2), zbank(m, 1), 0.0, C, A.max, A.mult).then_inc(S("sv", m), 1)
        V.tensor_scalar(col("ha", m, 3), zbank(m, 1), -C, 0.0, A.mult, A.max).then_inc(S("sv", m), 1)
        V.wait_ge(S("sa", m), 2)
        V.wait_ge(S("sv", m), 2)
        quant_tile("ha", "aqo", "aso", m, S("qa", m))
    if rank == 0:
        quant_in("xq", "xs", "xt", NC, 3 * NC, sem.lx1, sem.qx1)
    for m in range(MB):
        for i in range(2):
            if rank == 0:
                V.tensor_scalar(mask(m, i), zbank(m, i), 0.0, None, A.is_gt).then_inc(S("mk", m), 1)
            else:
                V.tensor_scalar(mask(m, 2 * i), zbank(m, i), 0.0, C, A.is_gt, A.mult).then_inc(S("mk", m), 1)
                V.tensor_scalar(mask(m, 2 * i + 1), zbank(m, i), 0.0, -C, A.is_lt, A.mult).then_inc(S("mk", m), 1)
    if rank == 0:
        quant_in("vq", "vs", "vt", 0, 256, sem.lv, sem.qv)
    for m in range(MB):
        V.wait_ge(S("mk", m), 2 if rank == 0 else 4)
        for i in range(2):
            V.wait_ge(S("u%d" % i, m), 1)
            if rank == 0:
                a = NC * (2 * m + i)
                V.tensor_tensor(T.yt[:, a:a + NC], ubank(m, i), mask(m, i), A.mult).then_inc(S("y%d" % i, m), 1)
                dq = (g.sync, g.scalar)[i]
                dq.wait_ge(S("y%d" % i, m), 1)
                dq.dma_start(T.y[:, a:a + NC], T.yt[:, a:a + NC]).then_inc(sem["st%d" % i], 16)
            else:
                for k in (2 * i, 2 * i + 1):
                    V.tensor_tensor(col("hb", m, k), ubank(m, i), mask(m, k), A.mult).then_inc(S("sb", m), 1)
        if rank > 0:
            V.wait_ge(S("sb", m), 4)
            quant_tile("hb", "bqo", "bso", m, S("qb", m))
    if rank == 0:
        g.sync.wait_ge(sem.st0, 16 * MB)
        g.scalar.wait_ge(sem.st1, 16 * MB)
